import numpy as np
import ml_dtypes


def mxq(x, axis, fmt="e4m3"):
    dtype, down = {"e4m3": (ml_dtypes.float8_e4m3fn, 7), "e5m2": (ml_dtypes.float8_e5m2, 14)}[fmt]
    v = np.moveaxis(np.asarray(x, np.float32).astype(ml_dtypes.bfloat16).astype(np.float64), axis, -1)
    blocks = v.reshape(v.shape[:-1] + (-1, 32))
    amax = np.abs(blocks).max(-1, keepdims=True)
    byte = np.maximum(np.where(amax > 0, np.frexp(amax)[1] - 1 + 127, 0) - down, 1)
    scale = np.exp2(byte - 127.0)
    codes = (blocks / scale).astype(np.float32).astype(dtype).astype(np.float64)
    return np.moveaxis((codes * scale).reshape(v.shape), -1, axis)


WIDE = False


def mx_kscale(k):
    if not WIDE:
        return np.ones(k)
    levels = np.array([10, -10, 5, -5, 0])
    if k % 512:
        return np.exp2(np.random.permutation(np.resize(levels, k // 32))).repeat(32)
    a = np.empty((k // 512, 16))
    for p in range(k // 512):
        a[p, :8] = np.random.permutation(np.resize(levels, 8))
        for g in range(8):
            far = levels[np.abs(levels - a[p, g]) >= 10]
            a[p, g + 8] = far[np.random.randint(len(far))]
    return np.exp2(a.ravel()).repeat(32)


def f64(x):
    return np.asarray(x).astype(np.float64)


def striped8(idx):
    return np.asarray(idx).reshape(8, -1, 16).transpose(0, 2, 1).reshape(128, -1).astype(np.uint16)


def unstriped8(offs):
    return offs.reshape(8, 16, -1).transpose(0, 2, 1).reshape(8, -1).astype(np.int64)


def pick8(x, idx, run):
    r = np.arange(len(x))
    return x[r[:, None], idx[r % (8 * run) // run]]


E2M1 = np.array([0.0, 0.5, 1.0, 1.5, 2.0, 3.0, 4.0, 6.0, -0.0, -0.5, -1.0, -1.5, -2.0, -3.0, -4.0, -6.0])


def pack_weight(w, fmt):
    k, n = w.shape
    w = f64(np.asarray(w, np.float32).astype(ml_dtypes.bfloat16)).reshape(k // 32, 32, n)
    amax = np.abs(w).max(1)
    if fmt == "e4m3":
        byte = np.frexp(amax)[1] - 1 + 127 - 7
    else:
        mant, ex = np.frexp(amax / 6.0)
        byte = np.where(mant > 0.5, ex, ex - 1) + 127
    byte = np.clip(np.where(amax > 0, byte, 1), 1, 254)
    scaled = (w * np.exp2(127.0 - byte)[:, None, :]).reshape(k, n).astype(np.float32)
    by_word = np.ascontiguousarray(scaled.reshape(k // 512, 128, 4, n).transpose(0, 1, 3, 2))
    if fmt == "e4m3":
        words = by_word.astype(ml_dtypes.float8_e4m3fn).view(np.uint8)
    else:
        c = by_word.astype(ml_dtypes.float4_e2m1fn).view(np.uint8) & 0xF
        words = (c[..., 0::2] | (c[..., 1::2] << 4)).reshape(k // 512, 128, 2 * n)
    return np.ascontiguousarray(words), np.ascontiguousarray(byte.astype(np.uint8).reshape(k // 512, 16, n))


def unpack_weight(words, scales, fmt):
    g, _, n = scales.shape
    words = np.ascontiguousarray(words).reshape(g, 128, n, -1)
    if fmt == "e4m3":
        vals = words.view(ml_dtypes.float8_e4m3fn).astype(np.float64)
    else:
        nib = np.empty((g, 128, n, 4), np.uint8)
        nib[..., 0::2] = words & 0xF
        nib[..., 1::2] = words >> 4
        vals = E2M1[nib]
    vals = vals * np.repeat(np.exp2(scales.astype(np.float64) - 127.0), 8, axis=1)[..., None]
    return vals.transpose(0, 1, 3, 2).reshape(g * 512, n)


D, T, I, Q = 512, 1024, 512, 128


def setup_inputs():
    n = np.random.standard_normal
    idx = np.stack([np.random.permutation(T)[:I] for _ in range(8)])
    idx2 = np.stack([np.random.permutation(T)[:I] for _ in range(8)])
    idx3 = np.stack([np.random.permutation(T)[:I] for _ in range(8)])
    idx4 = np.stack([np.random.permutation(T)[:I] for _ in range(8)])
    fd = mx_kscale(D)
    keysp = pack_weight(n((D, T)) / fd[:, None], "e2m1")
    return {
        "query": (n((D, Q)) * 0.9 / np.sqrt(D) * fd[:, None]).astype(np.float32),
        "keys_words": keysp[0],
        "keys_scales": keysp[1],
        "lam": (np.random.uniform(0.7, 1.3, (Q, 1))).astype(np.float32),
        "old": (1.0 * n((Q, T))).astype(np.float32),
        "offs": striped8(idx),
        "offs2": striped8(idx2),
        "offs3": striped8(idx3),
        "offs4": striped8(idx4),
    }


def reference(query, keys_words, keys_scales, lam, old, offs, offs2, offs3, offs4):
    idx = unstriped8(offs)
    idx2 = unstriped8(offs2)
    idx3 = unstriped8(offs3)
    idx4 = unstriped8(offs4)
    keysu = unpack_weight(keys_words, keys_scales, "e2m1")
    queryq = mxq(f64(query), 0, "e4m3")
    a = queryq.T @ keysu
    w = pick8(a, idx, 16) * f64(lam) - np.abs(pick8(a, idx2, 16) - pick8(a, idx3, 16))
    f1 = np.zeros((Q, T))
    f1[np.arange(Q)[:, None], idx[np.arange(Q) % 128 // 16]] = w
    f2 = f1 + f64(old)
    y = pick8(f2, idx4, 16)
    return y

@@ -1,0 +1,131 @@
+from contextlib import ExitStack
+
+import concourse.mybir as mybir
+
+D, T, I, Q = 512, 1024, 512, 128
+FLOPS = 2 * D * T * Q
+
+F32 = mybir.dt.float32
+BF16 = mybir.dt.bfloat16
+I32 = mybir.dt.int32
+U32 = mybir.dt.uint32
+U16 = mybir.dt.uint16
+U8 = mybir.dt.uint8
+FP8X4 = mybir.dt.float8_e4m3fn_x4
+FP4X4 = mybir.dt.float4_e2m1fn_x4
+ALU = mybir.AluOpType
+ACT = mybir.ActivationFunctionType
+
+P = 128
+PACK = 4
+N_TILE = 256
+HALF = I // 2
+GROUP = 16
+
+
+def tile_attend_betweentwo_lean_through_heads_kernel(
+    tc, query, keys_words, keys_scales, lam, old, offs, offs2, offs3, offs4, out
+):
+    nc = tc.nc
+    with ExitStack() as ctx:
+        keep = ctx.enter_context(tc.tile_pool(name="keep", bufs=1))
+        psum = ctx.enter_context(tc.psum_pool(name="psum", bufs=1))
+
+        list1 = keep.tile([P, I // GROUP], U16, name="list1")
+        list2 = keep.tile([P, I // GROUP], U16, name="list2")
+        list3 = keep.tile([P, I // GROUP], U16, name="list3")
+        list4 = keep.tile([P, I // GROUP], U16, name="list4")
+        q_raw = keep.tile([P, PACK, Q], F32, name="q_raw")
+        k_words = keep.tile([P, 2 * T], U8, name="k_words", align_bytes=64)
+        k_scales = keep.tile([P, T], U8, name="k_scales", align_bytes=64)
+        lam_col = keep.tile([P, 1], F32, name="lam_col")
+        old_sb = keep.tile([P, T], F32, name="old_sb")
+        f1 = keep.tile([P, T], F32, name="f1")
+
+        def entries(lst, h):
+            return lst[:, h * HALF // GROUP : (h + 1) * HALF // GROUP]
+
+        nc.vector.memset(k_scales[:].bitcast(I32), 0)
+        nc.sync.dma_start(out=q_raw[:], in_=query.rearrange("(p j) q -> p j q", j=PACK))
+        nc.gpsimd.dma_start(out=lam_col[:], in_=lam)
+        nc.sync.dma_start(out=k_words[:].bitcast(I32), in_=keys_words[0].bitcast(I32))
+        for quad in range(4):
+            nc.scalar.dma_start(
+                out=k_scales[32 * quad : 32 * quad + 4, :].bitcast(I32),
+                in_=keys_scales[0, 4 * quad : 4 * quad + 4, :].bitcast(I32),
+            )
+        nc.sync.dma_start(list1[:], offs)
+        nc.sync.dma_start(list3[:], offs3)
+        nc.sync.dma_start(list2[:], offs2)
+        nc.sync.dma_start(out=old_sb[:], in_=old)
+        nc.sync.dma_start(list4[:], offs4)
+        nc.gpsimd.memset(f1[:], 0.0)
+
+        q_bf = keep.tile([P, Q, PACK], BF16, name="q_bf", align_bytes=64)
+        q_codes = keep.tile([P, Q], U32, name="q_codes", align_bytes=64)
+        q_scales = keep.tile([P, Q], U8, name="q_scales", align_bytes=64)
+        halves = [slice(0, Q // 2), slice(Q // 2, Q)]
+        for cols in halves:
+            nc.vector.tensor_copy(
+                out=q_bf[:, cols, :].rearrange("p (c i) j -> p c j i", i=4),
+                in_=q_raw[:, :, cols].rearrange("p j (c i) -> p c j i", i=4),
+            )
+        for cols in halves:
+            nc.vector.quantize_mx(
+                out=q_codes[:, cols].bitcast(FP8X4),
+                scales=q_scales[:, cols],
+                in_=q_bf[:, cols, :].rearrange("p q j -> p (q j)"),
+            )
+
+        lam_wide = keep.tile([P, HALF], F32, name="lam_wide")
+        nc.scalar.activation(lam_wide[:], lam_col[:].to_broadcast([P, HALF]), ACT.Copy)
+
+        a = keep.tile([P, T], F32, name="a")
+        for c in range(T // N_TILE):
+            cols = slice(c * N_TILE, (c + 1) * N_TILE)
+            acc = psum.tile([Q, N_TILE], F32, name=f"acc{c}")
+            nc.tensor.matmul_mx(
+                out=acc[:],
+                lhsT=q_codes[:].bitcast(FP8X4),
+                lhsT_scale=q_scales[:],
+                rhs=k_words[:, 2 * c * N_TILE : 2 * (c + 1) * N_TILE].bitcast(FP4X4),
+                rhs_scale=k_scales[:, cols],
+                start=True,
+                stop=True,
+            )
+            if c % 2 == 0:
+                nc.scalar.copy(a[:, cols], acc[:])
+            else:
+                nc.vector.tensor_copy(out=a[:, cols], in_=acc[:])
+
+        def half_tile(name):
+            return keep.tile([P, HALF], F32, name=name)
+
+        third0, third1, second1 = half_tile("third0"), half_tile("third1"), half_tile("second1")
+        first1 = half_tile("first1")
+        scaled0, scaled1 = half_tile("scaled0"), half_tile("scaled1")
+        diff0, diff1 = half_tile("diff0"), half_tile("diff1")
+        neg0, neg1, abs1 = half_tile("neg0"), half_tile("neg1"), half_tile("abs1")
+
+        nc.scalar.activation(third0[:], a[:].indirect(entries(list3, 0)), ACT.Copy)
+        nc.vector.tensor_tensor(scaled0[:], a[:].indirect(entries(list1, 0)), lam_wide[:], ALU.mult)
+        nc.scalar.activation(third1[:], a[:].indirect(entries(list3, 1)), ACT.Copy)
+        nc.vector.tensor_tensor(diff0[:], a[:].indirect(entries(list2, 0)), third0[:], ALU.subtract)
+        nc.scalar.activation(second1[:], a[:].indirect(entries(list2, 1)), ACT.Copy)
+        nc.vector.scalar_tensor_tensor(neg0[:], diff0[:], -1.0, diff0[:], ALU.mult, ALU.min)
+        nc.vector.tensor_tensor(diff1[:], second1[:], third1[:], ALU.subtract)
+        nc.vector.tensor_tensor(f1[:].indirect(entries(list1, 0)), scaled0[:], neg0[:], ALU.add)
+        nc.scalar.activation(first1[:], a[:].indirect(entries(list1, 1)), ACT.Copy)
+        nc.scalar.activation(scaled1[:], first1[:], ACT.Copy, scale=lam_col[:])
+        nc.scalar.activation(abs1[:], diff1[:], ACT.Abs)
+        nc.scalar.activation(neg1[:], abs1[:], ACT.Copy, scale=-1.0)
+        nc.vector.tensor_tensor(f1[:].indirect(entries(list1, 1)), scaled1[:], neg1[:], ALU.add)
+
+        f2 = keep.tile([P, T], F32, name="f2")
+        nc.vector.tensor_tensor(f2[:], f1[:], old_sb[:], ALU.add)
+
+        res0, res1 = half_tile("res0"), half_tile("res1")
+        nc.vector.tensor_copy(res0[:], f2[:].indirect(entries(list4, 0)))
+        nc.scalar.activation(res1[:], f2[:].indirect(entries(list4, 1)), ACT.Copy)
+        nc.sync.dma_start(out=out[:, 0:HALF], in_=res0[:])
+        nc.scalar.dma_start(out=out[:, HALF:I], in_=res1[:])

@@ -47,19 +47,19 @@ def tile_attend_betweentwo_lean_through_heads_kernel(
 
         nc.vector.memset(k_scales[:].bitcast(I32), 0)
         nc.sync.dma_start(out=q_raw[:], in_=query.rearrange("(p j) q -> p j q", j=PACK))
-        nc.gpsimd.dma_start(out=lam_col[:], in_=lam)
         nc.sync.dma_start(out=k_words[:].bitcast(I32), in_=keys_words[0].bitcast(I32))
         for quad in range(4):
-            nc.scalar.dma_start(
+            nc.sync.dma_start(
                 out=k_scales[32 * quad : 32 * quad + 4, :].bitcast(I32),
                 in_=keys_scales[0, 4 * quad : 4 * quad + 4, :].bitcast(I32),
             )
-        nc.sync.dma_start(list1[:], offs)
+        nc.sync.dma_start(out=lam_col[:], in_=lam)
         nc.sync.dma_start(list3[:], offs3)
+        nc.sync.dma_start(list1[:], offs)
         nc.sync.dma_start(list2[:], offs2)
         nc.sync.dma_start(out=old_sb[:], in_=old)
         nc.sync.dma_start(list4[:], offs4)
-        nc.gpsimd.memset(f1[:], 0.0)
+        nc.vector.memset(f1[:], 0.0)
 
         q_bf = keep.tile([P, Q, PACK], BF16, name="q_bf", align_bytes=64)
         q_codes = keep.tile([P, Q], U32, name="q_codes", align_bytes=64)
@@ -81,14 +81,15 @@ def tile_attend_betweentwo_lean_through_heads_kernel(
         nc.scalar.activation(lam_wide[:], lam_col[:].to_broadcast([P, HALF]), ACT.Copy)
 
         a = keep.tile([P, T], F32, name="a")
-        for c in range(T // N_TILE):
-            cols = slice(c * N_TILE, (c + 1) * N_TILE)
-            acc = psum.tile([Q, N_TILE], F32, name=f"acc{c}")
+        edges = [0, 256, 512, 768, 896, 1024]
+        for c in range(len(edges) - 1):
+            cols = slice(edges[c], edges[c + 1])
+            acc = psum.tile([Q, edges[c + 1] - edges[c]], F32, name=f"acc{c}")
             nc.tensor.matmul_mx(
                 out=acc[:],
                 lhsT=q_codes[:].bitcast(FP8X4),
                 lhsT_scale=q_scales[:],
-                rhs=k_words[:, 2 * c * N_TILE : 2 * (c + 1) * N_TILE].bitcast(FP4X4),
+                rhs=k_words[:, 2 * edges[c] : 2 * edges[c + 1]].bitcast(FP4X4),
                 rhs_scale=k_scales[:, cols],
                 start=True,
                 stop=True,

from contextlib import ExitStack

import concourse.mybir as mybir

D, T, I, Q = 512, 1024, 512, 128
FLOPS = 2 * D * T * Q

F32 = mybir.dt.float32
BF16 = mybir.dt.bfloat16
I32 = mybir.dt.int32
U32 = mybir.dt.uint32
U16 = mybir.dt.uint16
U8 = mybir.dt.uint8
FP8X4 = mybir.dt.float8_e4m3fn_x4
FP4X4 = mybir.dt.float4_e2m1fn_x4
ALU = mybir.AluOpType
ACT = mybir.ActivationFunctionType

P = 128
PACK = 4
N_TILE = 256
HALF = I // 2
GROUP = 16


def tile_attend_betweentwo_lean_through_heads_kernel(
    tc, query, keys_words, keys_scales, lam, old, offs, offs2, offs3, offs4, out
):
    nc = tc.nc
    with ExitStack() as ctx:
        keep = ctx.enter_context(tc.tile_pool(name="keep", bufs=1))
        psum = ctx.enter_context(tc.psum_pool(name="psum", bufs=1))

        list1 = keep.tile([P, I // GROUP], U16, name="list1")
        list2 = keep.tile([P, I // GROUP], U16, name="list2")
        list3 = keep.tile([P, I // GROUP], U16, name="list3")
        list4 = keep.tile([P, I // GROUP], U16, name="list4")
        q_raw = keep.tile([P, PACK, Q], F32, name="q_raw")
        k_words = keep.tile([P, 2 * T], U8, name="k_words", align_bytes=64)
        k_scales = keep.tile([P, T], U8, name="k_scales", align_bytes=64)
        lam_col = keep.tile([P, 1], F32, name="lam_col")
        old_sb = keep.tile([P, T], F32, name="old_sb")
        f1 = keep.tile([P, T], F32, name="f1")

        def entries(lst, h):
            return lst[:, h * HALF // GROUP : (h + 1) * HALF // GROUP]

        nc.vector.memset(k_scales[:].bitcast(I32), 0)
        nc.sync.dma_start(out=q_raw[:], in_=query.rearrange("(p j) q -> p j q", j=PACK))
        nc.sync.dma_start(out=k_words[:].bitcast(I32), in_=keys_words[0].bitcast(I32))
        for quad in range(4):
            nc.sync.dma_start(
                out=k_scales[32 * quad : 32 * quad + 4, :].bitcast(I32),
                in_=keys_scales[0, 4 * quad : 4 * quad + 4, :].bitcast(I32),
            )
        nc.sync.dma_start(out=lam_col[:], in_=lam)
        nc.sync.dma_start(list3[:], offs3)
        nc.sync.dma_start(list1[:], offs)
        nc.sync.dma_start(list2[:], offs2)
        nc.sync.dma_start(out=old_sb[:], in_=old)
        nc.sync.dma_start(list4[:], offs4)
        nc.vector.memset(f1[:], 0.0)

        q_bf = keep.tile([P, Q, PACK], BF16, name="q_bf", align_bytes=64)
        q_codes = keep.tile([P, Q], U32, name="q_codes", align_bytes=64)
        q_scales = keep.tile([P, Q], U8, name="q_scales", align_bytes=64)
        halves = [slice(0, Q // 2), slice(Q // 2, Q)]
        for cols in halves:
            nc.vector.tensor_copy(
                out=q_bf[:, cols, :].rearrange("p (c i) j -> p c j i", i=4),
                in_=q_raw[:, :, cols].rearrange("p j (c i) -> p c j i", i=4),
            )
        for cols in halves:
            nc.vector.quantize_mx(
                out=q_codes[:, cols].bitcast(FP8X4),
                scales=q_scales[:, cols],
                in_=q_bf[:, cols, :].rearrange("p q j -> p (q j)"),
            )

        lam_wide = keep.tile([P, HALF], F32, name="lam_wide")
        nc.scalar.activation(lam_wide[:], lam_col[:].to_broadcast([P, HALF]), ACT.Copy)

        a = keep.tile([P, T], F32, name="a")
        edges = [0, 256, 512, 768, 896, 1024]
        for c in range(len(edges) - 1):
            cols = slice(edges[c], edges[c + 1])
            acc = psum.tile([Q, edges[c + 1] - edges[c]], F32, name=f"acc{c}")
            nc.tensor.matmul_mx(
                out=acc[:],
                lhsT=q_codes[:].bitcast(FP8X4),
                lhsT_scale=q_scales[:],
                rhs=k_words[:, 2 * edges[c] : 2 * edges[c + 1]].bitcast(FP4X4),
                rhs_scale=k_scales[:, cols],
                start=True,
                stop=True,
            )
            if c % 2 == 0:
                nc.scalar.copy(a[:, cols], acc[:])
            else:
                nc.vector.tensor_copy(out=a[:, cols], in_=acc[:])

        def half_tile(name):
            return keep.tile([P, HALF], F32, name=name)

        third0, third1, second1 = half_tile("third0"), half_tile("third1"), half_tile("second1")
        first1 = half_tile("first1")
        scaled0, scaled1 = half_tile("scaled0"), half_tile("scaled1")
        diff0, diff1 = half_tile("diff0"), half_tile("diff1")
        neg0, neg1, abs1 = half_tile("neg0"), half_tile("neg1"), half_tile("abs1")

        nc.scalar.activation(third0[:], a[:].indirect(entries(list3, 0)), ACT.Copy)
        nc.vector.tensor_tensor(scaled0[:], a[:].indirect(entries(list1, 0)), lam_wide[:], ALU.mult)
        nc.scalar.activation(third1[:], a[:].indirect(entries(list3, 1)), ACT.Copy)
        nc.vector.tensor_tensor(diff0[:], a[:].indirect(entries(list2, 0)), third0[:], ALU.subtract)
        nc.scalar.activation(second1[:], a[:].indirect(entries(list2, 1)), ACT.Copy)
        nc.vector.scalar_tensor_tensor(neg0[:], diff0[:], -1.0, diff0[:], ALU.mult, ALU.min)
        nc.vector.tensor_tensor(diff1[:], second1[:], third1[:], ALU.subtract)
        nc.vector.tensor_tensor(f1[:].indirect(entries(list1, 0)), scaled0[:], neg0[:], ALU.add)
        nc.scalar.activation(first1[:], a[:].indirect(entries(list1, 1)), ACT.Copy)
        nc.scalar.activation(scaled1[:], first1[:], ACT.Copy, scale=lam_col[:])
        nc.scalar.activation(abs1[:], diff1[:], ACT.Abs)
        nc.scalar.activation(neg1[:], abs1[:], ACT.Copy, scale=-1.0)
        nc.vector.tensor_tensor(f1[:].indirect(entries(list1, 1)), scaled1[:], neg1[:], ALU.add)

        f2 = keep.tile([P, T], F32, name="f2")
        nc.vector.tensor_tensor(f2[:], f1[:], old_sb[:], ALU.add)

        res0, res1 = half_tile("res0"), half_tile("res1")
        nc.vector.tensor_copy(res0[:], f2[:].indirect(entries(list4, 0)))
        nc.scalar.activation(res1[:], f2[:].indirect(entries(list4, 1)), ACT.Copy)
        nc.sync.dma_start(out=out[:, 0:HALF], in_=res0[:])
        nc.scalar.dma_start(out=out[:, HALF:I], in_=res1[:])
